import numpy as np
import ml_dtypes


def mxq(x, axis, fmt="e4m3"):
    dtype, down = {"e4m3": (ml_dtypes.float8_e4m3fn, 7), "e5m2": (ml_dtypes.float8_e5m2, 14)}[fmt]
    v = np.moveaxis(np.asarray(x, np.float32).astype(ml_dtypes.bfloat16).astype(np.float64), axis, -1)
    blocks = v.reshape(v.shape[:-1] + (-1, 32))
    amax = np.abs(blocks).max(-1, keepdims=True)
    byte = np.maximum(np.where(amax > 0, np.frexp(amax)[1] - 1 + 127, 0) - down, 1)
    scale = np.exp2(byte - 127.0)
    codes = (blocks / scale).astype(np.float32).astype(dtype).astype(np.float64)
    return np.moveaxis((codes * scale).reshape(v.shape), -1, axis)


WIDE = False


def mx_kscale(k, group=512):
    if not WIDE:
        return np.ones(k)
    levels = np.array([10, -10, 5, -5, 0])
    if group != 512:
        return np.exp2(np.random.permutation(np.resize(levels, k // group))).repeat(group)
    if k % 512:
        return np.exp2(np.random.permutation(np.resize(levels, k // 32))).repeat(32)
    a = np.empty((k // 512, 16))
    for p in range(k // 512):
        a[p, :8] = np.random.permutation(np.resize(levels, 8))
        for g in range(8):
            far = levels[np.abs(levels - a[p, g]) >= 10]
            a[p, g + 8] = far[np.random.randint(len(far))]
    return np.exp2(a.ravel()).repeat(32)


def f64(x):
    return np.asarray(x).astype(np.float64)


def striped(idx):
    return np.tile(np.asarray(idx).reshape(-1, 16).T, (8, 1)).astype(np.uint16)


def unstriped(offs):
    return offs[:16].T.reshape(-1).astype(np.int64)


H, KV, D, NQ, N = 4, 4, 256, 512, 512
CAP = 2.0


def setup_inputs():
    n = np.random.standard_normal
    s = mx_kscale(D, 0)[:, None]
    u = mx_kscale(N)
    t = np.random.uniform(0.5, 2.0, N) * u
    v = n((KV, N, 128))
    return {
        "qT": (n((H, D, NQ)) * s * (0.70 / np.sqrt(D))).astype(np.float32),
        "kT": (n((KV, D, N)) / s).astype(np.float32),
        "t": t.reshape(N, 1).astype(np.float32),
        "v": (v / t[:, None]).astype(np.float32),
        "mask": (np.arange(N)[:, None] <= np.sort(np.random.randint(N // 4, N, NQ))[None, :]).astype(np.float32),
    }


def reference(qT, kT, t, v, mask):
    a = mxq(f64(kT), 1, "e4m3").transpose(0, 2, 1) @ mxq(f64(qT), 1, "e4m3")
    a = CAP * np.tanh(a / CAP)
    p = np.maximum(a, 0.0)
    p = p * f64(mask)
    w = p * f64(t)
    y = mxq(w, 1, "e4m3").transpose(0, 2, 1) @ mxq(f64(v), 1, "e4m3")
    y = y / 16.0
    return y

@@ -1,0 +1,278 @@
+from contextlib import ExitStack
+
+import concourse.mybir as mybir
+
+H, D, NQ, N, E = 4, 256, 512, 512, 128
+CAP = 2.0
+OUT_SCALE = 1.0 / 16.0
+FLOPS = 2 * H * N * NQ * (D + E)
+
+F32 = mybir.dt.float32
+BF16 = mybir.dt.bfloat16
+U32 = mybir.dt.uint32
+U8 = mybir.dt.uint8
+FP8X4 = mybir.dt.float8_e4m3fn_x4
+ALU = mybir.AluOpType
+ACT = mybir.ActivationFunctionType
+
+P = 128
+PACK = 4
+ROWS = D // PACK
+QC = 128
+SCORE_BANKS = 3
+
+
+def tile_rows_a_relu_mask_cap_kernel(tc, qT, kT, t, v, mask, out):
+    nc = tc.nc
+    copy_on = {"V": nc.vector.tensor_copy, "S": nc.scalar.copy}
+
+    with ExitStack() as ctx:
+        sb = ctx.enter_context(tc.tile_pool(name="sb", bufs=1))
+        ps = ctx.enter_context(tc.psum_pool(name="ps", bufs=1))
+
+        def tiles(name, count, shape, dtype):
+            return [sb.tile(shape, dtype, name=name + str(i), align_bytes=64) for i in range(count)]
+
+        k_raw = tiles("k_raw", 2, [P, PACK, N], F32)
+        q_raw = tiles("q_raw", 2, [P, PACK, NQ], F32)
+        v_raw = tiles("v_raw", 2, [P, 2, PACK, E], F32)
+        mask_raw = sb.tile([P, PACK, NQ], F32, name="mask_raw")
+        t_raw = sb.tile([P, PACK], F32, name="t_raw")
+        t_cap = sb.tile([P, PACK], F32, name="t_cap")
+        gain = sb.tile([P, NQ, PACK], F32, name="gain")
+        k_bf = tiles("k_bf", 2, [P, N * PACK], BF16)
+        q_bf = tiles("q_bf", 2, [P, NQ * PACK], BF16)
+        v_bf = tiles("v_bf", 2, [P, 2 * E * PACK], BF16)
+        w_bf = tiles("w_bf", H, [P, NQ * PACK], BF16)
+        k_code, k_scale = tiles("k_code", 2, [P, N], U32), tiles("k_scale", 2, [P, N], U8)
+        q_code, q_scale = tiles("q_code", 2, [P, NQ], U32), tiles("q_scale", 2, [P, NQ], U8)
+        v_code, v_scale = tiles("v_code", 2, [P, 2 * E], U32), tiles("v_scale", 2, [P, 2 * E], U8)
+        w_code, w_scale = tiles("w_code", H, [P, NQ], U32), tiles("w_scale", H, [P, NQ], U8)
+        capped = tiles("capped", H, [P, NQ * PACK], F32)
+        y_sb = tiles("y_sb", H, [P, NQ // QC, E], F32)
+        score_ps = [[ps.tile([P, PACK, QC], F32, name="score%d_%d" % (g, b)) for b in range(SCORE_BANKS)] for g in range(2)]
+        y_ps = [ps.tile([P, PACK, E], F32, name="y%d" % b) for b in range(2)]
+
+        def load_k(pair, lo, hi):
+            src = kT[2 * pair : 2 * pair + 2].rearrange("g (p j) i -> (g p) j i", j=PACK)
+            nc.sync.dma_start(out=k_raw[pair][:, :, lo:hi], in_=src[:, :, lo:hi])
+
+        def load_q(pair, lo, hi):
+            src = qT[2 * pair : 2 * pair + 2].rearrange("g (p j) q -> (g p) j q", j=PACK)
+            nc.sync.dma_start(out=q_raw[pair][:, :, lo:hi], in_=src[:, :, lo:hi])
+
+        def load_mask(lo, hi):
+            src = mask.rearrange("(p j) q -> p j q", j=PACK)
+            nc.sync.dma_start(out=mask_raw[:, :, lo:hi], in_=src[:, :, lo:hi])
+
+        def load_v(pair):
+            src = v[2 * pair : 2 * pair + 2].rearrange("g (p j) e -> p g j e", j=PACK)
+            nc.sync.dma_start(out=v_raw[pair][:], in_=src)
+
+        def pack_k(eng, pair, lo, hi):
+            dst = k_bf[pair][:].rearrange("p (r s j) -> p s j r", r=PACK, j=PACK)
+            src = k_raw[pair][:].rearrange("p j (s r) -> p s j r", r=PACK)
+            copy_on[eng](out=dst[:, lo // PACK : hi // PACK], in_=src[:, lo // PACK : hi // PACK])
+
+        def pack_q(eng, pair, lo, hi):
+            dst = q_bf[pair][:].rearrange("p (c i j) -> p c j i", i=PACK, j=PACK)
+            src = q_raw[pair][:].rearrange("p j (c i) -> p c j i", i=PACK)
+            copy_on[eng](out=dst[:, lo // PACK : hi // PACK], in_=src[:, lo // PACK : hi // PACK])
+
+        def pack_v(eng, head):
+            pair, g = divmod(head, 2)
+            dst = v_bf[pair][:, g * E * PACK : (g + 1) * E * PACK].rearrange("p (c i j) -> p c j i", i=PACK, j=PACK)
+            src = v_raw[pair][:, g].rearrange("p j (c i) -> p c j i", i=PACK)
+            copy_on[eng](out=dst, in_=src)
+
+        def quantize(code, scale, bf, lo, hi):
+            nc.vector.quantize_mx(out=code[:, lo:hi].bitcast(FP8X4), scales=scale[:, lo:hi], in_=bf[:, PACK * lo : PACK * hi])
+
+        def quant_k(pair, lo, hi):
+            quantize(k_code[pair], k_scale[pair], k_bf[pair], lo, hi)
+
+        def quant_q(pair, lo, hi):
+            quantize(q_code[pair], q_scale[pair], q_bf[pair], lo, hi)
+
+        def quant_v(pair):
+            quantize(v_code[pair], v_scale[pair], v_bf[pair], 0, 2 * E)
+
+        def quant_w(head, lo, hi):
+            quantize(w_code[head], w_scale[head], w_bf[head], lo, hi)
+
+        def make_gain(lo, hi):
+            dst = gain[:].rearrange("p (c i) j -> p c j i", i=PACK)[:, lo // PACK : hi // PACK]
+            src = mask_raw[:].rearrange("p j (c i) -> p c j i", i=PACK)[:, lo // PACK : hi // PACK]
+            factor = t_cap[:].unsqueeze(1).unsqueeze(3).broadcast_to([P, (hi - lo) // PACK, PACK, PACK])
+            nc.vector.tensor_tensor(out=dst, in0=src, in1=factor, op=ALU.mult)
+
+        def score_bank(head, c):
+            pair, g = divmod(head, 2)
+            return score_ps[g][(pair * (NQ // QC) + c) % SCORE_BANKS]
+
+        def scores(head, c):
+            pair, g = divmod(head, 2)
+            rows = slice(g * ROWS, (g + 1) * ROWS)
+            cols = slice(c * QC, (c + 1) * QC)
+            for r in range(PACK):
+                toks = slice(r * P, (r + 1) * P)
+                nc.tensor.matmul_mx(
+                    out=score_bank(head, c)[:, r, :],
+                    lhsT=k_code[pair][rows, toks].bitcast(FP8X4),
+                    lhsT_scale=k_scale[pair][rows, toks],
+                    rhs=q_code[pair][rows, cols].bitcast(FP8X4),
+                    rhs_scale=q_scale[pair][rows, cols],
+                    start=True,
+                    stop=True,
+                )
+
+        def cap(head, c):
+            dst = capped[head][:, c * QC * PACK : (c + 1) * QC * PACK].rearrange("p (q r) -> p q r", r=PACK)
+            nc.scalar.activation(out=dst, in_=score_bank(head, c)[:].rearrange("p r q -> p q r"), func=ACT.Tanh, scale=1.0 / CAP)
+
+        def weigh(head, c):
+            cols = slice(c * QC * PACK, (c + 1) * QC * PACK)
+            nc.vector.scalar_tensor_tensor(
+                out=w_bf[head][:, cols],
+                in0=capped[head][:, cols],
+                scalar=0.0,
+                in1=gain[:].rearrange("p q j -> p (q j)")[:, cols],
+                op0=ALU.max,
+                op1=ALU.mult,
+            )
+
+        def values(head, c_lo, c_hi, bank):
+            pair, g = divmod(head, 2)
+            feats = slice(g * E, (g + 1) * E)
+            for c in range(c_lo, c_hi):
+                cols = slice(c * QC, (c + 1) * QC)
+                nc.tensor.matmul_mx(
+                    out=y_ps[bank][:, c, :],
+                    lhsT=w_code[head][:, cols].bitcast(FP8X4),
+                    lhsT_scale=w_scale[head][:, cols],
+                    rhs=v_code[pair][:, feats].bitcast(FP8X4),
+                    rhs_scale=v_scale[pair][:, feats],
+                    start=True,
+                    stop=True,
+                )
+
+        def emit(eng, head, c_lo, c_hi, bank):
+            if eng == "S":
+                nc.scalar.activation(out=y_sb[head][:, c_lo:c_hi, :], in_=y_ps[bank][:, c_lo:c_hi, :], func=ACT.Copy, scale=OUT_SCALE)
+            else:
+                nc.vector.tensor_scalar_mul(y_sb[head][:, c_lo:c_hi, :], y_ps[bank][:, c_lo:c_hi, :], OUT_SCALE)
+            dst = out[head].rearrange("(c p) e -> p c e", p=P)
+            nc.sync.dma_start(out=dst[:, c_lo:c_hi, :], in_=y_sb[head][:, c_lo:c_hi, :])
+
+        ctx.enter_context(tc.manual_schedule())
+        nc.sync.dma_start(out=t_raw[:], in_=t.rearrange("(p j) o -> p (j o)", j=PACK))
+        nc.gpsimd.tensor_scalar(out=t_cap[:], in0=t_raw[:], scalar1=CAP, scalar2=0.0, op0=ALU.mult, op1=ALU.add)
+        load_q(0, 0, 128)
+        load_k(0, 0, 256)
+        load_k(0, 256, 512)
+        load_q(0, 128, 256)
+        load_mask(0, 256)
+        load_q(0, 256, 512)
+        load_mask(256, 512)
+        load_k(1, 0, 512)
+        load_q(1, 0, 256)
+        load_v(0)
+        load_q(1, 256, 512)
+        load_v(1)
+        pack_q("V", 0, 0, 128)
+        pack_k("S", 0, 0, 128)
+        pack_k("V", 0, 128, 256)
+        quant_q(0, 0, 128)
+        pack_k("S", 0, 256, 336)
+        pack_k("V", 0, 336, 512)
+        quant_k(0, 0, 256)
+        quant_k(0, 256, 512)
+        scores(0, 0)
+        scores(1, 0)
+        pack_q("V", 0, 128, 256)
+        cap(0, 0)
+        cap(1, 0)
+        make_gain(0, 128)
+        quant_q(0, 128, 256)
+        scores(0, 1)
+        scores(1, 1)
+        weigh(0, 0)
+        pack_q("V", 0, 256, 512)
+        cap(0, 1)
+        cap(1, 1)
+        weigh(1, 0)
+        quant_q(0, 256, 512)
+        scores(0, 2)
+        scores(1, 2)
+        cap(0, 2)
+        cap(1, 2)
+        scores(0, 3)
+        scores(1, 3)
+        cap(0, 3)
+        cap(1, 3)
+        make_gain(128, 256)
+        weigh(0, 1)
+        weigh(1, 1)
+        make_gain(256, 512)
+        quant_w(0, 0, 256)
+        quant_w(1, 0, 256)
+        pack_k("S", 1, 0, 512)
+        weigh(0, 2)
+        weigh(1, 2)
+        pack_q("S", 1, 0, 256)
+        weigh(0, 3)
+        quant_k(1, 0, 512)
+        weigh(1, 3)
+        quant_q(1, 0, 256)
+        scores(2, 0)
+        scores(3, 0)
+        scores(2, 1)
+        scores(3, 1)
+        pack_v("S", 0)
+        pack_v("S", 1)
+        quant_w(0, 256, 512)
+        quant_w(1, 256, 512)
+        cap(2, 0)
+        cap(2, 1)
+        pack_q("V", 1, 256, 512)
+        quant_v(0)
+        values(0, 0, 4, 0)
+        values(1, 0, 4, 1)
+        quant_q(1, 256, 512)
+        scores(2, 2)
+        scores(3, 2)
+        cap(3, 0)
+        cap(3, 1)
+        weigh(2, 0)
+        weigh(2, 1)
+        scores(2, 3)
+        scores(3, 3)
+        emit("S", 0, 0, 4, 0)
+        cap(2, 2)
+        cap(2, 3)
+        pack_v("V", 2)
+        quant_w(2, 0, 256)
+        pack_v("V", 3)
+        weigh(3, 0)
+        quant_v(1)
+        weigh(3, 1)
+        values(2, 0, 2, 0)
+        cap(3, 2)
+        cap(3, 3)
+        emit("S", 1, 0, 4, 1)
+        weigh(2, 2)
+        quant_w(3, 0, 256)
+        values(3, 0, 2, 1)
+        emit("S", 2, 0, 2, 0)
+        emit("S", 3, 0, 2, 1)
+        weigh(2, 3)
+        weigh(3, 2)
+        quant_w(2, 256, 512)
+        values(2, 2, 4, 0)
+        emit("S", 2, 2, 4, 0)
+        weigh(3, 3)
+        quant_w(3, 256, 384)
+        values(3, 2, 3, 1)
+        quant_w(3, 384, 512)
+        values(3, 3, 4, 1)
+        emit("S", 3, 2, 4, 1)

@@ -110,21 +110,21 @@ def tile_rows_a_relu_mask_cap_kernel(tc, qT, kT, t, v, mask, out):
             pair, g = divmod(head, 2)
             return score_ps[g][(pair * (NQ // QC) + c) % SCORE_BANKS]
 
-        def scores(head, c):
-            pair, g = divmod(head, 2)
-            rows = slice(g * ROWS, (g + 1) * ROWS)
+        def scores2(pair, c):
             cols = slice(c * QC, (c + 1) * QC)
             for r in range(PACK):
                 toks = slice(r * P, (r + 1) * P)
-                nc.tensor.matmul_mx(
-                    out=score_bank(head, c)[:, r, :],
-                    lhsT=k_code[pair][rows, toks].bitcast(FP8X4),
-                    lhsT_scale=k_scale[pair][rows, toks],
-                    rhs=q_code[pair][rows, cols].bitcast(FP8X4),
-                    rhs_scale=q_scale[pair][rows, cols],
-                    start=True,
-                    stop=True,
-                )
+                for g in range(2):
+                    rows = slice(g * ROWS, (g + 1) * ROWS)
+                    nc.tensor.matmul_mx(
+                        out=score_bank(2 * pair + g, c)[:, r, :],
+                        lhsT=k_code[pair][rows, toks].bitcast(FP8X4),
+                        lhsT_scale=k_scale[pair][rows, toks],
+                        rhs=q_code[pair][rows, cols].bitcast(FP8X4),
+                        rhs_scale=q_scale[pair][rows, cols],
+                        start=True,
+                        stop=True,
+                    )
 
         def cap(head, c):
             dst = capped[head][:, c * QC * PACK : (c + 1) * QC * PACK].rearrange("p (q r) -> p q r", r=PACK)
@@ -167,112 +167,108 @@ def tile_rows_a_relu_mask_cap_kernel(tc, qT, kT, t, v, mask, out):
         ctx.enter_context(tc.manual_schedule())
         nc.sync.dma_start(out=t_raw[:], in_=t.rearrange("(p j) o -> p (j o)", j=PACK))
         nc.gpsimd.tensor_scalar(out=t_cap[:], in0=t_raw[:], scalar1=CAP, scalar2=0.0, op0=ALU.mult, op1=ALU.add)
-        load_q(0, 0, 128)
-        load_k(0, 0, 256)
-        load_k(0, 256, 512)
-        load_q(0, 128, 256)
-        load_mask(0, 256)
-        load_q(0, 256, 512)
-        load_mask(256, 512)
-        load_k(1, 0, 512)
-        load_q(1, 0, 256)
-        load_v(0)
-        load_q(1, 256, 512)
-        load_v(1)
-        pack_q("V", 0, 0, 128)
-        pack_k("S", 0, 0, 128)
+        load_k(0, 0, 512)
+        pack_k("V", 0, 384, 512)
         pack_k("V", 0, 128, 256)
-        quant_q(0, 0, 128)
-        pack_k("S", 0, 256, 336)
-        pack_k("V", 0, 336, 512)
+        load_q(0, 0, 256)
+        pack_k("S", 0, 0, 128)
+        load_mask(0, 256)
+        pack_k("S", 0, 256, 384)
+        pack_q("S", 0, 0, 128)
         quant_k(0, 0, 256)
         quant_k(0, 256, 512)
-        scores(0, 0)
-        scores(1, 0)
-        pack_q("V", 0, 128, 256)
+        load_q(0, 256, 512)
+        load_q(1, 0, 512)
+        quant_q(0, 0, 128)
+        pack_q("S", 0, 128, 256)
+        quant_q(0, 128, 256)
+        scores2(0, 0)
+        make_gain(0, 128)
+        make_gain(128, 256)
+        pack_q("V", 0, 384, 512)
+        load_mask(256, 512)
         cap(0, 0)
         cap(1, 0)
-        make_gain(0, 128)
-        quant_q(0, 128, 256)
-        scores(0, 1)
-        scores(1, 1)
+        scores2(0, 1)
         weigh(0, 0)
-        pack_q("V", 0, 256, 512)
+        weigh(1, 0)
+        pack_q("S", 0, 256, 384)
+        quant_q(0, 256, 512)
+        scores2(0, 3)
         cap(0, 1)
         cap(1, 1)
-        weigh(1, 0)
-        quant_q(0, 256, 512)
-        scores(0, 2)
-        scores(1, 2)
-        cap(0, 2)
-        cap(1, 2)
-        scores(0, 3)
-        scores(1, 3)
-        cap(0, 3)
-        cap(1, 3)
-        make_gain(128, 256)
+        pack_q("S", 1, 128, 256)
         weigh(0, 1)
         weigh(1, 1)
-        make_gain(256, 512)
+        pack_q("V", 1, 0, 128)
+        make_gain(384, 512)
+        pack_q("S", 1, 256, 384)
+        make_gain(256, 384)
+        load_k(1, 0, 512)
         quant_w(0, 0, 256)
-        quant_w(1, 0, 256)
-        pack_k("S", 1, 0, 512)
-        weigh(0, 2)
-        weigh(1, 2)
-        pack_q("S", 1, 0, 256)
-        weigh(0, 3)
-        quant_k(1, 0, 512)
+        cap(1, 3)
+        cap(0, 3)
         weigh(1, 3)
+        scores2(0, 2)
         quant_q(1, 0, 256)
-        scores(2, 0)
-        scores(3, 0)
-        scores(2, 1)
-        scores(3, 1)
-        pack_v("S", 0)
+        pack_q("S", 1, 384, 512)
+        weigh(0, 3)
+        cap(1, 2)
+        pack_k("V", 1, 384, 512)
+        pack_k("V", 1, 128, 256)
+        cap(0, 2)
+        quant_w(1, 0, 256)
+        load_v(0)
+        pack_k("S", 1, 0, 128)
+        pack_k("S", 1, 256, 384)
+        quant_k(1, 0, 512)
+        weigh(1, 2)
         pack_v("S", 1)
-        quant_w(0, 256, 512)
-        quant_w(1, 256, 512)
-        cap(2, 0)
-        cap(2, 1)
-        pack_q("V", 1, 256, 512)
-        quant_v(0)
-        values(0, 0, 4, 0)
-        values(1, 0, 4, 1)
-        quant_q(1, 256, 512)
-        scores(2, 2)
-        scores(3, 2)
+        scores2(1, 0)
+        load_v(1)
+        pack_v("S", 0)
+        pack_v("S", 2)
+        scores2(1, 1)
         cap(3, 0)
+        weigh(0, 2)
+        quant_v(0)
+        quant_w(1, 256, 512)
+        cap(2, 1)
+        cap(2, 0)
+        quant_w(0, 256, 512)
+        quant_q(1, 256, 512)
         cap(3, 1)
-        weigh(2, 0)
-        weigh(2, 1)
-        scores(2, 3)
-        scores(3, 3)
-        emit("S", 0, 0, 4, 0)
-        cap(2, 2)
-        cap(2, 3)
-        pack_v("V", 2)
-        quant_w(2, 0, 256)
-        pack_v("V", 3)
         weigh(3, 0)
-        quant_v(1)
+        scores2(1, 2)
+        weigh(2, 1)
+        cap(2, 2)
+        weigh(2, 0)
+        pack_v("S", 3)
         weigh(3, 1)
-        values(2, 0, 2, 0)
+        values(1, 0, 4, 1)
+        scores2(1, 3)
+        quant_w(2, 0, 256)
         cap(3, 2)
+        quant_w(3, 0, 256)
         cap(3, 3)
         emit("S", 1, 0, 4, 1)
-        weigh(2, 2)
-        quant_w(3, 0, 256)
-        values(3, 0, 2, 1)
-        emit("S", 2, 0, 2, 0)
-        emit("S", 3, 0, 2, 1)
-        weigh(2, 3)
+        values(0, 0, 4, 0)
+        quant_v(1)
         weigh(3, 2)
-        quant_w(2, 256, 512)
-        values(2, 2, 4, 0)
-        emit("S", 2, 2, 4, 0)
+        cap(2, 3)
+        weigh(2, 2)
+        values(3, 0, 2, 1)
+        emit("S", 0, 0, 4, 0)
+        values(2, 0, 2, 0)
         weigh(3, 3)
-        quant_w(3, 256, 384)
-        values(3, 2, 3, 1)
+        weigh(2, 3)
         quant_w(3, 384, 512)
+        quant_w(3, 256, 384)
+        emit("S", 3, 0, 2, 1)
         values(3, 3, 4, 1)
+        quant_w(2, 256, 512)
+        emit("S", 2, 0, 2, 0)
+        values(3, 2, 3, 1)
         emit("S", 3, 2, 4, 1)
+        values(2, 2, 4, 0)
+        emit("V", 2, 2, 4, 0)

@@ -19,7 +19,7 @@ P = 128
 PACK = 4
 ROWS = D // PACK
 QC = 128
-SCORE_BANKS = 3
+SCORE_BANKS = 2
 
 
 def tile_rows_a_relu_mask_cap_kernel(tc, qT, kT, t, v, mask, out):
@@ -51,7 +51,7 @@ def tile_rows_a_relu_mask_cap_kernel(tc, qT, kT, t, v, mask, out):
         capped = tiles("capped", H, [P, NQ * PACK], F32)
         y_sb = tiles("y_sb", H, [P, NQ // QC, E], F32)
         score_ps = [[ps.tile([P, PACK, QC], F32, name="score%d_%d" % (g, b)) for b in range(SCORE_BANKS)] for g in range(2)]
-        y_ps = [ps.tile([P, PACK, E], F32, name="y%d" % b) for b in range(2)]
+        y_ps = [ps.tile([P, PACK, E], F32, name="y%d" % b) for b in range(H)]
 
         def load_k(pair, lo, hi):
             src = kT[2 * pair : 2 * pair + 2].rearrange("g (p j) i -> (g p) j i", j=PACK)
@@ -130,8 +130,8 @@ def tile_rows_a_relu_mask_cap_kernel(tc, qT, kT, t, v, mask, out):
             dst = capped[head][:, c * QC * PACK : (c + 1) * QC * PACK].rearrange("p (q r) -> p q r", r=PACK)
             nc.scalar.activation(out=dst, in_=score_bank(head, c)[:].rearrange("p r q -> p q r"), func=ACT.Tanh, scale=1.0 / CAP)
 
-        def weigh(head, c):
-            cols = slice(c * QC * PACK, (c + 1) * QC * PACK)
+        def weigh(head, c_lo, c_hi):
+            cols = slice(c_lo * QC * PACK, c_hi * QC * PACK)
             nc.vector.scalar_tensor_tensor(
                 out=w_bf[head][:, cols],
                 in0=capped[head][:, cols],
@@ -165,110 +165,94 @@ def tile_rows_a_relu_mask_cap_kernel(tc, qT, kT, t, v, mask, out):
             nc.sync.dma_start(out=dst[:, c_lo:c_hi, :], in_=y_sb[head][:, c_lo:c_hi, :])
 
         ctx.enter_context(tc.manual_schedule())
-        nc.sync.dma_start(out=t_raw[:], in_=t.rearrange("(p j) o -> p (j o)", j=PACK))
+        nc.scalar.dma_start(out=t_raw[:], in_=t.rearrange("(p j) o -> p (j o)", j=PACK))
         nc.gpsimd.tensor_scalar(out=t_cap[:], in0=t_raw[:], scalar1=CAP, scalar2=0.0, op0=ALU.mult, op1=ALU.add)
         load_k(0, 0, 512)
-        pack_k("V", 0, 384, 512)
-        pack_k("V", 0, 128, 256)
         load_q(0, 0, 256)
-        pack_k("S", 0, 0, 128)
         load_mask(0, 256)
-        pack_k("S", 0, 256, 384)
-        pack_q("S", 0, 0, 128)
-        quant_k(0, 0, 256)
-        quant_k(0, 256, 512)
         load_q(0, 256, 512)
-        load_q(1, 0, 512)
+        load_mask(256, 512)
+        load_q(1, 0, 256)
+        load_k(1, 0, 512)
+        load_v(0)
+        load_q(1, 256, 512)
+        load_v(1)
+        pack_k("S", 0, 0, 192)
+        pack_k("V", 0, 192, 512)
+        quant_k(0, 0, 256)
+        pack_q("V", 0, 0, 64)
+        quant_k(0, 256, 512)
+        pack_q("S", 0, 64, 128)
         quant_q(0, 0, 128)
+        scores2(0, 0)
         pack_q("S", 0, 128, 256)
         quant_q(0, 128, 256)
-        scores2(0, 0)
-        make_gain(0, 128)
-        make_gain(128, 256)
-        pack_q("V", 0, 384, 512)
-        load_mask(256, 512)
-        cap(0, 0)
-        cap(1, 0)
         scores2(0, 1)
-        weigh(0, 0)
-        weigh(1, 0)
+        cap(0, 0)
+        make_gain(0, 256)
+        pack_q("V", 0, 384, 512)
         pack_q("S", 0, 256, 384)
+        weigh(0, 0, 1)
+        cap(1, 0)
         quant_q(0, 256, 512)
-        scores2(0, 3)
-        cap(0, 1)
+        scores2(0, 2)
+        make_gain(256, 512)
         cap(1, 1)
-        pack_q("S", 1, 128, 256)
-        weigh(0, 1)
-        weigh(1, 1)
-        pack_q("V", 1, 0, 128)
-        make_gain(384, 512)
-        pack_q("S", 1, 256, 384)
-        make_gain(256, 384)
-        load_k(1, 0, 512)
-        quant_w(0, 0, 256)
+        cap(0, 1)
+        scores2(0, 3)
+        weigh(1, 0, 2)
+        cap(0, 2)
+        weigh(0, 1, 3)
+        pack_q("S", 1, 0, 256)
+        pack_k("V", 1, 0, 512)
+        quant_q(1, 0, 256)
+        quant_k(1, 0, 512)
+        cap(1, 2)
         cap(1, 3)
         cap(0, 3)
-        weigh(1, 3)
-        scores2(0, 2)
-        quant_q(1, 0, 256)
-        pack_q("S", 1, 384, 512)
-        weigh(0, 3)
-        cap(1, 2)
-        pack_k("V", 1, 384, 512)
-        pack_k("V", 1, 128, 256)
-        cap(0, 2)
-        quant_w(1, 0, 256)
-        load_v(0)
-        pack_k("S", 1, 0, 128)
-        pack_k("S", 1, 256, 384)
-        quant_k(1, 0, 512)
-        weigh(1, 2)
-        pack_v("S", 1)
         scores2(1, 0)
-        load_v(1)
-        pack_v("S", 0)
-        pack_v("S", 2)
         scores2(1, 1)
-        cap(3, 0)
-        weigh(0, 2)
-        quant_v(0)
-        quant_w(1, 256, 512)
-        cap(2, 1)
+        pack_v("S", 0)
+        pack_v("S", 1)
+        weigh(1, 2, 4)
+        pack_q("S", 1, 256, 512)
         cap(2, 0)
-        quant_w(0, 256, 512)
+        weigh(0, 3, 4)
+        cap(3, 0)
+        cap(2, 1)
+        quant_w(1, 0, 512)
         quant_q(1, 256, 512)
-        cap(3, 1)
-        weigh(3, 0)
         scores2(1, 2)
-        weigh(2, 1)
-        cap(2, 2)
-        weigh(2, 0)
-        pack_v("S", 3)
-        weigh(3, 1)
-        values(1, 0, 4, 1)
+        cap(3, 1)
+        quant_v(0)
+        quant_w(0, 0, 512)
+        weigh(2, 0, 2)
+        pack_v("S", 2)
         scores2(1, 3)
-        quant_w(2, 0, 256)
         cap(3, 2)
-        quant_w(3, 0, 256)
-        cap(3, 3)
-        emit("S", 1, 0, 4, 1)
+        weigh(3, 0, 2)
         values(0, 0, 4, 0)
+        cap(3, 3)
+        values(1, 0, 4, 1)
+        pack_v("S", 3)
+        quant_w(2, 0, 256)
+        weigh(3, 2, 4)
         quant_v(1)
-        weigh(3, 2)
-        cap(2, 3)
-        weigh(2, 2)
-        values(3, 0, 2, 1)
+        cap(2, 2)
+        quant_w(3, 0, 512)
+        values(2, 0, 2, 2)
         emit("S", 0, 0, 4, 0)
-        values(2, 0, 2, 0)
-        weigh(3, 3)
-        weigh(2, 3)
-        quant_w(3, 384, 512)
-        quant_w(3, 256, 384)
-        emit("S", 3, 0, 2, 1)
-        values(3, 3, 4, 1)
-        quant_w(2, 256, 512)
-        emit("S", 2, 0, 2, 0)
-        values(3, 2, 3, 1)
-        emit("S", 3, 2, 4, 1)
-        values(2, 2, 4, 0)
-        emit("V", 2, 2, 4, 0)
+        weigh(2, 2, 3)
+        emit("S", 1, 0, 4, 1)
+        cap(2, 3)
+        emit("S", 2, 0, 2, 2)
+        weigh(2, 3, 4)
+        values(3, 0, 4, 3)
+        quant_w(2, 256, 384)
+        emit("S", 3, 0, 2, 3)
+        values(2, 2, 3, 0)
+        quant_w(2, 384, 512)
+        emit("S", 3, 2, 4, 3)
+        emit("V", 2, 2, 3, 0)
+        values(2, 3, 4, 1)
+        emit("S", 2, 3, 4, 1)

@@ -172,17 +172,16 @@ def tile_rows_a_relu_mask_cap_kernel(tc, qT, kT, t, v, mask, out):
         load_mask(0, 256)
         load_q(0, 256, 512)
         load_mask(256, 512)
-        load_q(1, 0, 256)
         load_k(1, 0, 512)
-        load_v(0)
+        load_q(1, 0, 256)
         load_q(1, 256, 512)
+        load_v(0)
         load_v(1)
-        pack_k("S", 0, 0, 192)
-        pack_k("V", 0, 192, 512)
-        quant_k(0, 0, 256)
+        pack_k("V", 0, 0, 256)
+        pack_k("S", 0, 256, 512)
         pack_q("V", 0, 0, 64)
-        quant_k(0, 256, 512)
         pack_q("S", 0, 64, 128)
+        quant_k(0, 0, 512)
         quant_q(0, 0, 128)
         scores2(0, 0)
         pack_q("S", 0, 128, 256)
@@ -190,69 +189,71 @@ def tile_rows_a_relu_mask_cap_kernel(tc, qT, kT, t, v, mask, out):
         scores2(0, 1)
         cap(0, 0)
         make_gain(0, 256)
-        pack_q("V", 0, 384, 512)
-        pack_q("S", 0, 256, 384)
-        weigh(0, 0, 1)
         cap(1, 0)
-        quant_q(0, 256, 512)
-        scores2(0, 2)
-        make_gain(256, 512)
+        pack_q("S", 0, 448, 512)
+        pack_q("V", 0, 256, 384)
+        pack_q("V", 0, 384, 448)
         cap(1, 1)
+        quant_q(0, 256, 384)
+        weigh(1, 0, 1)
+        scores2(0, 2)
         cap(0, 1)
+        quant_q(0, 384, 512)
+        make_gain(256, 512)
+        weigh(0, 0, 2)
         scores2(0, 3)
-        weigh(1, 0, 2)
-        cap(0, 2)
-        weigh(0, 1, 3)
-        pack_q("S", 1, 0, 256)
-        pack_k("V", 1, 0, 512)
-        quant_q(1, 0, 256)
-        quant_k(1, 0, 512)
         cap(1, 2)
+        cap(0, 2)
         cap(1, 3)
+        weigh(1, 1, 4)
+        pack_q("V", 1, 0, 256)
+        pack_k("S", 1, 0, 512)
+        quant_k(1, 0, 512)
         cap(0, 3)
+        pack_q("S", 1, 256, 512)
+        quant_q(1, 0, 256)
         scores2(1, 0)
         scores2(1, 1)
-        pack_v("S", 0)
-        pack_v("S", 1)
-        weigh(1, 2, 4)
-        pack_q("S", 1, 256, 512)
-        cap(2, 0)
-        weigh(0, 3, 4)
-        cap(3, 0)
-        cap(2, 1)
         quant_w(1, 0, 512)
+        weigh(0, 2, 4)
+        pack_v("V", 1)
+        pack_v("S", 0)
         quant_q(1, 256, 512)
-        scores2(1, 2)
-        cap(3, 1)
-        quant_v(0)
         quant_w(0, 0, 512)
-        weigh(2, 0, 2)
-        pack_v("S", 2)
+        cap(2, 0)
+        cap(3, 0)
+        scores2(1, 2)
+        cap(2, 1)
+        cap(3, 1)
         scores2(1, 3)
-        cap(3, 2)
+        quant_v(0)
+        pack_v("S", 2)
+        weigh(2, 0, 2)
         weigh(3, 0, 2)
-        values(0, 0, 4, 0)
-        cap(3, 3)
-        values(1, 0, 4, 1)
         pack_v("S", 3)
+        values(0, 0, 4, 0)
+        values(1, 0, 4, 1)
+        cap(3, 2)
+        cap(3, 3)
+        quant_v(1)
         quant_w(2, 0, 256)
         weigh(3, 2, 4)
-        quant_v(1)
-        cap(2, 2)
-        quant_w(3, 0, 512)
-        values(2, 0, 2, 2)
         emit("S", 0, 0, 4, 0)
-        weigh(2, 2, 3)
         emit("S", 1, 0, 4, 1)
+        cap(2, 2)
+        values(2, 0, 2, 2)
         cap(2, 3)
+        quant_w(3, 0, 256)
+        quant_w(3, 256, 512)
         emit("S", 2, 0, 2, 2)
+        weigh(2, 2, 3)
         weigh(2, 3, 4)
         values(3, 0, 4, 3)
         quant_w(2, 256, 384)
-        emit("S", 3, 0, 2, 3)
-        values(2, 2, 3, 0)
         quant_w(2, 384, 512)
-        emit("S", 3, 2, 4, 3)
-        emit("V", 2, 2, 3, 0)
+        values(2, 2, 3, 0)
         values(2, 3, 4, 1)
-        emit("S", 2, 3, 4, 1)
+        emit("S", 3, 0, 2, 3)
+        emit("S", 3, 2, 4, 3)
+        emit("S", 2, 2, 3, 0)
+        emit("V", 2, 3, 4, 1)

@@ -17,8 +17,11 @@ ACT = mybir.ActivationFunctionType
 
 P = 128
 PACK = 4
+LINE = 4
 ROWS = D // PACK
+PAIRS = H // 2
 QC = 128
+CHUNKS = NQ // QC
 SCORE_BANKS = 2
 
 
@@ -33,25 +36,25 @@ def tile_rows_a_relu_mask_cap_kernel(tc, qT, kT, t, v, mask, out):
         def tiles(name, count, shape, dtype):
             return [sb.tile(shape, dtype, name=name + str(i), align_bytes=64) for i in range(count)]
 
-        k_raw = tiles("k_raw", 2, [P, PACK, N], F32)
-        q_raw = tiles("q_raw", 2, [P, PACK, NQ], F32)
-        v_raw = tiles("v_raw", 2, [P, 2, PACK, E], F32)
+        k_raw = tiles("k_raw", PAIRS, [P, PACK, N], F32)
+        q_raw = tiles("q_raw", PAIRS, [P, PACK, NQ], F32)
+        v_raw = tiles("v_raw", PAIRS, [P, 2, PACK, E], F32)
         mask_raw = sb.tile([P, PACK, NQ], F32, name="mask_raw")
         t_raw = sb.tile([P, PACK], F32, name="t_raw")
         t_cap = sb.tile([P, PACK], F32, name="t_cap")
         gain = sb.tile([P, NQ, PACK], F32, name="gain")
-        k_bf = tiles("k_bf", 2, [P, N * PACK], BF16)
-        q_bf = tiles("q_bf", 2, [P, NQ * PACK], BF16)
-        v_bf = tiles("v_bf", 2, [P, 2 * E * PACK], BF16)
+        k_bf = tiles("k_bf", PAIRS, [P, N * PACK], BF16)
+        q_bf = tiles("q_bf", PAIRS, [P, NQ * PACK], BF16)
+        v_bf = tiles("v_bf", PAIRS, [P, 2 * E * PACK], BF16)
         w_bf = tiles("w_bf", H, [P, NQ * PACK], BF16)
-        k_code, k_scale = tiles("k_code", 2, [P, N], U32), tiles("k_scale", 2, [P, N], U8)
-        q_code, q_scale = tiles("q_code", 2, [P, NQ], U32), tiles("q_scale", 2, [P, NQ], U8)
-        v_code, v_scale = tiles("v_code", 2, [P, 2 * E], U32), tiles("v_scale", 2, [P, 2 * E], U8)
+        k_code, k_scale = tiles("k_code", PAIRS, [P, N], U32), tiles("k_scale", PAIRS, [P, N], U8)
+        q_code, q_scale = tiles("q_code", PAIRS, [P, NQ], U32), tiles("q_scale", PAIRS, [P, NQ], U8)
+        v_code, v_scale = tiles("v_code", PAIRS, [P, 2 * E], U32), tiles("v_scale", PAIRS, [P, 2 * E], U8)
         w_code, w_scale = tiles("w_code", H, [P, NQ], U32), tiles("w_scale", H, [P, NQ], U8)
         capped = tiles("capped", H, [P, NQ * PACK], F32)
-        y_sb = tiles("y_sb", H, [P, NQ // QC, E], F32)
+        y_sb = tiles("y_sb", H, [P, CHUNKS, E], F32)
         score_ps = [[ps.tile([P, PACK, QC], F32, name="score%d_%d" % (g, b)) for b in range(SCORE_BANKS)] for g in range(2)]
-        y_ps = [ps.tile([P, PACK, E], F32, name="y%d" % b) for b in range(H)]
+        y_ps = [ps.tile([P, CHUNKS, E], F32, name="y%d" % b) for b in range(H)]
 
         def load_k(pair, lo, hi):
             src = kT[2 * pair : 2 * pair + 2].rearrange("g (p j) i -> (g p) j i", j=PACK)
@@ -75,14 +78,14 @@ def tile_rows_a_relu_mask_cap_kernel(tc, qT, kT, t, v, mask, out):
             copy_on[eng](out=dst[:, lo // PACK : hi // PACK], in_=src[:, lo // PACK : hi // PACK])
 
         def pack_q(eng, pair, lo, hi):
-            dst = q_bf[pair][:].rearrange("p (c i j) -> p c j i", i=PACK, j=PACK)
-            src = q_raw[pair][:].rearrange("p j (c i) -> p c j i", i=PACK)
-            copy_on[eng](out=dst[:, lo // PACK : hi // PACK], in_=src[:, lo // PACK : hi // PACK])
+            dst = q_bf[pair][:].rearrange("p (c i j) -> p c j i", i=LINE, j=PACK)
+            src = q_raw[pair][:].rearrange("p j (c i) -> p c j i", i=LINE)
+            copy_on[eng](out=dst[:, lo // LINE : hi // LINE], in_=src[:, lo // LINE : hi // LINE])
 
         def pack_v(eng, head):
             pair, g = divmod(head, 2)
-            dst = v_bf[pair][:, g * E * PACK : (g + 1) * E * PACK].rearrange("p (c i j) -> p c j i", i=PACK, j=PACK)
-            src = v_raw[pair][:, g].rearrange("p j (c i) -> p c j i", i=PACK)
+            dst = v_bf[pair][:, g * E * PACK : (g + 1) * E * PACK].rearrange("p (c i j) -> p c j i", i=LINE, j=PACK)
+            src = v_raw[pair][:, g].rearrange("p j (c i) -> p c j i", i=LINE)
             copy_on[eng](out=dst, in_=src)
 
         def quantize(code, scale, bf, lo, hi):
@@ -101,16 +104,15 @@ def tile_rows_a_relu_mask_cap_kernel(tc, qT, kT, t, v, mask, out):
             quantize(w_code[head], w_scale[head], w_bf[head], lo, hi)
 
         def make_gain(lo, hi):
-            dst = gain[:].rearrange("p (c i) j -> p c j i", i=PACK)[:, lo // PACK : hi // PACK]
-            src = mask_raw[:].rearrange("p j (c i) -> p c j i", i=PACK)[:, lo // PACK : hi // PACK]
-            factor = t_cap[:].unsqueeze(1).unsqueeze(3).broadcast_to([P, (hi - lo) // PACK, PACK, PACK])
+            dst = gain[:].rearrange("p (c i) j -> p c j i", i=LINE)[:, lo // LINE : hi // LINE]
+            src = mask_raw[:].rearrange("p j (c i) -> p c j i", i=LINE)[:, lo // LINE : hi // LINE]
+            factor = t_cap[:].unsqueeze(1).unsqueeze(3).broadcast_to([P, (hi - lo) // LINE, PACK, LINE])
             nc.vector.tensor_tensor(out=dst, in0=src, in1=factor, op=ALU.mult)
 
         def score_bank(head, c):
-            pair, g = divmod(head, 2)
-            return score_ps[g][(pair * (NQ // QC) + c) % SCORE_BANKS]
+            return score_ps[head % 2][c % SCORE_BANKS]
 
-        def scores2(pair, c):
+        def scores(pair, c):
             cols = slice(c * QC, (c + 1) * QC)
             for r in range(PACK):
                 toks = slice(r * P, (r + 1) * P)
@@ -126,7 +128,7 @@ def tile_rows_a_relu_mask_cap_kernel(tc, qT, kT, t, v, mask, out):
                         stop=True,
                     )
 
-        def cap(head, c):
+        def squash(head, c):
             dst = capped[head][:, c * QC * PACK : (c + 1) * QC * PACK].rearrange("p (q r) -> p q r", r=PACK)
             nc.scalar.activation(out=dst, in_=score_bank(head, c)[:].rearrange("p r q -> p q r"), func=ACT.Tanh, scale=1.0 / CAP)
 
@@ -141,7 +143,7 @@ def tile_rows_a_relu_mask_cap_kernel(tc, qT, kT, t, v, mask, out):
                 op1=ALU.mult,
             )
 
-        def values(head, c_lo, c_hi, bank):
+        def mix(head, c_lo, c_hi, bank):
             pair, g = divmod(head, 2)
             feats = slice(g * E, (g + 1) * E)
             for c in range(c_lo, c_hi):
@@ -165,8 +167,8 @@ def tile_rows_a_relu_mask_cap_kernel(tc, qT, kT, t, v, mask, out):
             nc.sync.dma_start(out=dst[:, c_lo:c_hi, :], in_=y_sb[head][:, c_lo:c_hi, :])
 
         ctx.enter_context(tc.manual_schedule())
+
         nc.scalar.dma_start(out=t_raw[:], in_=t.rearrange("(p j) o -> p (j o)", j=PACK))
-        nc.gpsimd.tensor_scalar(out=t_cap[:], in0=t_raw[:], scalar1=CAP, scalar2=0.0, op0=ALU.mult, op1=ALU.add)
         load_k(0, 0, 512)
         load_q(0, 0, 256)
         load_mask(0, 256)
@@ -174,86 +176,93 @@ def tile_rows_a_relu_mask_cap_kernel(tc, qT, kT, t, v, mask, out):
         load_mask(256, 512)
         load_k(1, 0, 512)
         load_q(1, 0, 256)
-        load_q(1, 256, 512)
         load_v(0)
+        load_q(1, 256, 512)
         load_v(1)
+
         pack_k("V", 0, 0, 256)
+        nc.vector.tensor_scalar_mul(t_cap[:], t_raw[:], CAP)
         pack_k("S", 0, 256, 512)
-        pack_q("V", 0, 0, 64)
-        pack_q("S", 0, 64, 128)
+        pack_q("V", 0, 128, 192)
         quant_k(0, 0, 512)
+        pack_q("S", 0, 0, 128)
         quant_q(0, 0, 128)
-        scores2(0, 0)
-        pack_q("S", 0, 128, 256)
+        pack_q("S", 0, 192, 256)
         quant_q(0, 128, 256)
-        scores2(0, 1)
-        cap(0, 0)
+        scores(0, 0)
+        scores(0, 1)
         make_gain(0, 256)
-        cap(1, 0)
-        pack_q("S", 0, 448, 512)
+        squash(0, 0)
+        squash(1, 0)
+
         pack_q("V", 0, 256, 384)
-        pack_q("V", 0, 384, 448)
-        cap(1, 1)
+        pack_q("S", 0, 384, 512)
+        weigh(0, 0, 1)
         quant_q(0, 256, 384)
         weigh(1, 0, 1)
-        scores2(0, 2)
-        cap(0, 1)
+        squash(0, 1)
+        scores(0, 2)
+        squash(1, 1)
         quant_q(0, 384, 512)
+        scores(0, 3)
+        squash(0, 2)
+        squash(1, 2)
+        squash(0, 3)
         make_gain(256, 512)
-        weigh(0, 0, 2)
-        scores2(0, 3)
-        cap(1, 2)
-        cap(0, 2)
-        cap(1, 3)
-        weigh(1, 1, 4)
-        pack_q("V", 1, 0, 256)
-        pack_k("S", 1, 0, 512)
-        quant_k(1, 0, 512)
-        cap(0, 3)
-        pack_q("S", 1, 256, 512)
-        quant_q(1, 0, 256)
-        scores2(1, 0)
-        scores2(1, 1)
-        quant_w(1, 0, 512)
+        weigh(0, 1, 2)
+
+        pack_k("S", 1, 0, 128)
+        pack_k("V", 1, 128, 512)
         weigh(0, 2, 4)
-        pack_v("V", 1)
+        squash(1, 3)
+        pack_q("S", 1, 0, 256)
+        quant_k(1, 0, 512)
+        quant_q(1, 0, 256)
         pack_v("S", 0)
-        quant_q(1, 256, 512)
+        pack_v("S", 1)
+        weigh(1, 1, 4)
+        scores(1, 0)
+        scores(1, 1)
+        pack_q("S", 1, 256, 512)
+
+        squash(2, 0)
         quant_w(0, 0, 512)
-        cap(2, 0)
-        cap(3, 0)
-        scores2(1, 2)
-        cap(2, 1)
-        cap(3, 1)
-        scores2(1, 3)
         quant_v(0)
+        mix(0, 0, 4, 0)
+        squash(2, 1)
+        squash(3, 0)
+        quant_q(1, 256, 512)
+        quant_w(1, 0, 512)
+        squash(3, 1)
         pack_v("S", 2)
         weigh(2, 0, 2)
-        weigh(3, 0, 2)
-        pack_v("S", 3)
-        values(0, 0, 4, 0)
-        values(1, 0, 4, 1)
-        cap(3, 2)
-        cap(3, 3)
-        quant_v(1)
-        quant_w(2, 0, 256)
-        weigh(3, 2, 4)
+        weigh(3, 0, 1)
+        scores(1, 2)
+        squash(3, 2)
         emit("S", 0, 0, 4, 0)
+        quant_w(2, 0, 256)
+        scores(1, 3)
+        weigh(3, 1, 3)
+        mix(1, 0, 4, 1)
+        squash(3, 3)
+        pack_v("S", 3)
+        weigh(3, 3, 4)
+        quant_v(1)
+        quant_w(3, 0, 512)
+        mix(2, 0, 2, 2)
         emit("S", 1, 0, 4, 1)
-        cap(2, 2)
-        values(2, 0, 2, 2)
-        cap(2, 3)
-        quant_w(3, 0, 256)
-        quant_w(3, 256, 512)
-        emit("S", 2, 0, 2, 2)
+        mix(3, 0, 4, 3)
+
+        squash(2, 2)
         weigh(2, 2, 3)
+        squash(2, 3)
         weigh(2, 3, 4)
-        values(3, 0, 4, 3)
         quant_w(2, 256, 384)
-        quant_w(2, 384, 512)
-        values(2, 2, 3, 0)
-        values(2, 3, 4, 1)
+        emit("S", 2, 0, 2, 2)
         emit("S", 3, 0, 2, 3)
+        mix(2, 2, 3, 0)
         emit("S", 3, 2, 4, 3)
         emit("S", 2, 2, 3, 0)
+        quant_w(2, 384, 512)
+        mix(2, 3, 4, 1)
         emit("V", 2, 3, 4, 1)

from contextlib import ExitStack

import concourse.mybir as mybir

H, D, NQ, N, E = 4, 256, 512, 512, 128
CAP = 2.0
OUT_SCALE = 1.0 / 16.0
FLOPS = 2 * H * N * NQ * (D + E)

F32 = mybir.dt.float32
BF16 = mybir.dt.bfloat16
U32 = mybir.dt.uint32
U8 = mybir.dt.uint8
FP8X4 = mybir.dt.float8_e4m3fn_x4
ALU = mybir.AluOpType
ACT = mybir.ActivationFunctionType

P = 128
PACK = 4
LINE = 4
ROWS = D // PACK
PAIRS = H // 2
QC = 128
CHUNKS = NQ // QC
SCORE_BANKS = 2


def tile_rows_a_relu_mask_cap_kernel(tc, qT, kT, t, v, mask, out):
    nc = tc.nc
    copy_on = {"V": nc.vector.tensor_copy, "S": nc.scalar.copy}

    with ExitStack() as ctx:
        sb = ctx.enter_context(tc.tile_pool(name="sb", bufs=1))
        ps = ctx.enter_context(tc.psum_pool(name="ps", bufs=1))

        def tiles(name, count, shape, dtype):
            return [sb.tile(shape, dtype, name=name + str(i), align_bytes=64) for i in range(count)]

        k_raw = tiles("k_raw", PAIRS, [P, PACK, N], F32)
        q_raw = tiles("q_raw", PAIRS, [P, PACK, NQ], F32)
        v_raw = tiles("v_raw", PAIRS, [P, 2, PACK, E], F32)
        mask_raw = sb.tile([P, PACK, NQ], F32, name="mask_raw")
        t_raw = sb.tile([P, PACK], F32, name="t_raw")
        t_cap = sb.tile([P, PACK], F32, name="t_cap")
        gain = sb.tile([P, NQ, PACK], F32, name="gain")
        k_bf = tiles("k_bf", PAIRS, [P, N * PACK], BF16)
        q_bf = tiles("q_bf", PAIRS, [P, NQ * PACK], BF16)
        v_bf = tiles("v_bf", PAIRS, [P, 2 * E * PACK], BF16)
        w_bf = tiles("w_bf", H, [P, NQ * PACK], BF16)
        k_code, k_scale = tiles("k_code", PAIRS, [P, N], U32), tiles("k_scale", PAIRS, [P, N], U8)
        q_code, q_scale = tiles("q_code", PAIRS, [P, NQ], U32), tiles("q_scale", PAIRS, [P, NQ], U8)
        v_code, v_scale = tiles("v_code", PAIRS, [P, 2 * E], U32), tiles("v_scale", PAIRS, [P, 2 * E], U8)
        w_code, w_scale = tiles("w_code", H, [P, NQ], U32), tiles("w_scale", H, [P, NQ], U8)
        capped = tiles("capped", H, [P, NQ * PACK], F32)
        y_sb = tiles("y_sb", H, [P, CHUNKS, E], F32)
        score_ps = [[ps.tile([P, PACK, QC], F32, name="score%d_%d" % (g, b)) for b in range(SCORE_BANKS)] for g in range(2)]
        y_ps = [ps.tile([P, CHUNKS, E], F32, name="y%d" % b) for b in range(H)]

        def load_k(pair, lo, hi):
            src = kT[2 * pair : 2 * pair + 2].rearrange("g (p j) i -> (g p) j i", j=PACK)
            nc.sync.dma_start(out=k_raw[pair][:, :, lo:hi], in_=src[:, :, lo:hi])

        def load_q(pair, lo, hi):
            src = qT[2 * pair : 2 * pair + 2].rearrange("g (p j) q -> (g p) j q", j=PACK)
            nc.sync.dma_start(out=q_raw[pair][:, :, lo:hi], in_=src[:, :, lo:hi])

        def load_mask(lo, hi):
            src = mask.rearrange("(p j) q -> p j q", j=PACK)
            nc.sync.dma_start(out=mask_raw[:, :, lo:hi], in_=src[:, :, lo:hi])

        def load_v(pair):
            src = v[2 * pair : 2 * pair + 2].rearrange("g (p j) e -> p g j e", j=PACK)
            nc.sync.dma_start(out=v_raw[pair][:], in_=src)

        def pack_k(eng, pair, lo, hi):
            dst = k_bf[pair][:].rearrange("p (r s j) -> p s j r", r=PACK, j=PACK)
            src = k_raw[pair][:].rearrange("p j (s r) -> p s j r", r=PACK)
            copy_on[eng](out=dst[:, lo // PACK : hi // PACK], in_=src[:, lo // PACK : hi // PACK])

        def pack_q(eng, pair, lo, hi):
            dst = q_bf[pair][:].rearrange("p (c i j) -> p c j i", i=LINE, j=PACK)
            src = q_raw[pair][:].rearrange("p j (c i) -> p c j i", i=LINE)
            copy_on[eng](out=dst[:, lo // LINE : hi // LINE], in_=src[:, lo // LINE : hi // LINE])

        def pack_v(eng, head):
            pair, g = divmod(head, 2)
            dst = v_bf[pair][:, g * E * PACK : (g + 1) * E * PACK].rearrange("p (c i j) -> p c j i", i=LINE, j=PACK)
            src = v_raw[pair][:, g].rearrange("p j (c i) -> p c j i", i=LINE)
            copy_on[eng](out=dst, in_=src)

        def quantize(code, scale, bf, lo, hi):
            nc.vector.quantize_mx(out=code[:, lo:hi].bitcast(FP8X4), scales=scale[:, lo:hi], in_=bf[:, PACK * lo : PACK * hi])

        def quant_k(pair, lo, hi):
            quantize(k_code[pair], k_scale[pair], k_bf[pair], lo, hi)

        def quant_q(pair, lo, hi):
            quantize(q_code[pair], q_scale[pair], q_bf[pair], lo, hi)

        def quant_v(pair):
            quantize(v_code[pair], v_scale[pair], v_bf[pair], 0, 2 * E)

        def quant_w(head, lo, hi):
            quantize(w_code[head], w_scale[head], w_bf[head], lo, hi)

        def make_gain(lo, hi):
            dst = gain[:].rearrange("p (c i) j -> p c j i", i=LINE)[:, lo // LINE : hi // LINE]
            src = mask_raw[:].rearrange("p j (c i) -> p c j i", i=LINE)[:, lo // LINE : hi // LINE]
            factor = t_cap[:].unsqueeze(1).unsqueeze(3).broadcast_to([P, (hi - lo) // LINE, PACK, LINE])
            nc.vector.tensor_tensor(out=dst, in0=src, in1=factor, op=ALU.mult)

        def score_bank(head, c):
            return score_ps[head % 2][c % SCORE_BANKS]

        def scores(pair, c):
            cols = slice(c * QC, (c + 1) * QC)
            for r in range(PACK):
                toks = slice(r * P, (r + 1) * P)
                for g in range(2):
                    rows = slice(g * ROWS, (g + 1) * ROWS)
                    nc.tensor.matmul_mx(
                        out=score_bank(2 * pair + g, c)[:, r, :],
                        lhsT=k_code[pair][rows, toks].bitcast(FP8X4),
                        lhsT_scale=k_scale[pair][rows, toks],
                        rhs=q_code[pair][rows, cols].bitcast(FP8X4),
                        rhs_scale=q_scale[pair][rows, cols],
                        start=True,
                        stop=True,
                    )

        def squash(head, c):
            dst = capped[head][:, c * QC * PACK : (c + 1) * QC * PACK].rearrange("p (q r) -> p q r", r=PACK)
            nc.scalar.activation(out=dst, in_=score_bank(head, c)[:].rearrange("p r q -> p q r"), func=ACT.Tanh, scale=1.0 / CAP)

        def weigh(head, c_lo, c_hi):
            cols = slice(c_lo * QC * PACK, c_hi * QC * PACK)
            nc.vector.scalar_tensor_tensor(
                out=w_bf[head][:, cols],
                in0=capped[head][:, cols],
                scalar=0.0,
                in1=gain[:].rearrange("p q j -> p (q j)")[:, cols],
                op0=ALU.max,
                op1=ALU.mult,
            )

        def mix(head, c_lo, c_hi, bank):
            pair, g = divmod(head, 2)
            feats = slice(g * E, (g + 1) * E)
            for c in range(c_lo, c_hi):
                cols = slice(c * QC, (c + 1) * QC)
                nc.tensor.matmul_mx(
                    out=y_ps[bank][:, c, :],
                    lhsT=w_code[head][:, cols].bitcast(FP8X4),
                    lhsT_scale=w_scale[head][:, cols],
                    rhs=v_code[pair][:, feats].bitcast(FP8X4),
                    rhs_scale=v_scale[pair][:, feats],
                    start=True,
                    stop=True,
                )

        def emit(eng, head, c_lo, c_hi, bank):
            if eng == "S":
                nc.scalar.activation(out=y_sb[head][:, c_lo:c_hi, :], in_=y_ps[bank][:, c_lo:c_hi, :], func=ACT.Copy, scale=OUT_SCALE)
            else:
                nc.vector.tensor_scalar_mul(y_sb[head][:, c_lo:c_hi, :], y_ps[bank][:, c_lo:c_hi, :], OUT_SCALE)
            dst = out[head].rearrange("(c p) e -> p c e", p=P)
            nc.sync.dma_start(out=dst[:, c_lo:c_hi, :], in_=y_sb[head][:, c_lo:c_hi, :])

        ctx.enter_context(tc.manual_schedule())

        nc.scalar.dma_start(out=t_raw[:], in_=t.rearrange("(p j) o -> p (j o)", j=PACK))
        load_k(0, 0, 512)
        load_q(0, 0, 256)
        load_mask(0, 256)
        load_q(0, 256, 512)
        load_mask(256, 512)
        load_k(1, 0, 512)
        load_q(1, 0, 256)
        load_v(0)
        load_q(1, 256, 512)
        load_v(1)

        pack_k("V", 0, 0, 256)
        nc.vector.tensor_scalar_mul(t_cap[:], t_raw[:], CAP)
        pack_k("S", 0, 256, 512)
        pack_q("V", 0, 128, 192)
        quant_k(0, 0, 512)
        pack_q("S", 0, 0, 128)
        quant_q(0, 0, 128)
        pack_q("S", 0, 192, 256)
        quant_q(0, 128, 256)
        scores(0, 0)
        scores(0, 1)
        make_gain(0, 256)
        squash(0, 0)
        squash(1, 0)

        pack_q("V", 0, 256, 384)
        pack_q("S", 0, 384, 512)
        weigh(0, 0, 1)
        quant_q(0, 256, 384)
        weigh(1, 0, 1)
        squash(0, 1)
        scores(0, 2)
        squash(1, 1)
        quant_q(0, 384, 512)
        scores(0, 3)
        squash(0, 2)
        squash(1, 2)
        squash(0, 3)
        make_gain(256, 512)
        weigh(0, 1, 2)

        pack_k("S", 1, 0, 128)
        pack_k("V", 1, 128, 512)
        weigh(0, 2, 4)
        squash(1, 3)
        pack_q("S", 1, 0, 256)
        quant_k(1, 0, 512)
        quant_q(1, 0, 256)
        pack_v("S", 0)
        pack_v("S", 1)
        weigh(1, 1, 4)
        scores(1, 0)
        scores(1, 1)
        pack_q("S", 1, 256, 512)

        squash(2, 0)
        quant_w(0, 0, 512)
        quant_v(0)
        mix(0, 0, 4, 0)
        squash(2, 1)
        squash(3, 0)
        quant_q(1, 256, 512)
        quant_w(1, 0, 512)
        squash(3, 1)
        pack_v("S", 2)
        weigh(2, 0, 2)
        weigh(3, 0, 1)
        scores(1, 2)
        squash(3, 2)
        emit("S", 0, 0, 4, 0)
        quant_w(2, 0, 256)
        scores(1, 3)
        weigh(3, 1, 3)
        mix(1, 0, 4, 1)
        squash(3, 3)
        pack_v("S", 3)
        weigh(3, 3, 4)
        quant_v(1)
        quant_w(3, 0, 512)
        mix(2, 0, 2, 2)
        emit("S", 1, 0, 4, 1)
        mix(3, 0, 4, 3)

        squash(2, 2)
        weigh(2, 2, 3)
        squash(2, 3)
        weigh(2, 3, 4)
        quant_w(2, 256, 384)
        emit("S", 2, 0, 2, 2)
        emit("S", 3, 0, 2, 3)
        mix(2, 2, 3, 0)
        emit("S", 3, 2, 4, 3)
        emit("S", 2, 2, 3, 0)
        quant_w(2, 384, 512)
        mix(2, 3, 4, 1)
        emit("V", 2, 3, 4, 1)
